import numpy as np
import ml_dtypes


def mxq(x, axis, fmt="e4m3"):
    dtype, down = {"e4m3": (ml_dtypes.float8_e4m3fn, 7), "e5m2": (ml_dtypes.float8_e5m2, 14)}[fmt]
    v = np.moveaxis(np.asarray(x, np.float32).astype(ml_dtypes.bfloat16).astype(np.float64), axis, -1)
    blocks = v.reshape(v.shape[:-1] + (-1, 32))
    amax = np.abs(blocks).max(-1, keepdims=True)
    byte = np.maximum(np.where(amax > 0, np.frexp(amax)[1] - 1 + 127, 0) - down, 1)
    scale = np.exp2(byte - 127.0)
    codes = (blocks / scale).astype(np.float32).astype(dtype).astype(np.float64)
    return np.moveaxis((codes * scale).reshape(v.shape), -1, axis)


WIDE = False


def mx_kscale(k):
    if not WIDE:
        return np.ones(k)
    levels = np.array([10, -10, 5, -5, 0])
    if k % 512:
        return np.exp2(np.random.permutation(np.resize(levels, k // 32))).repeat(32)
    a = np.empty((k // 512, 16))
    for p in range(k // 512):
        a[p, :8] = np.random.permutation(np.resize(levels, 8))
        for g in range(8):
            far = levels[np.abs(levels - a[p, g]) >= 10]
            a[p, g + 8] = far[np.random.randint(len(far))]
    return np.exp2(a.ravel()).repeat(32)


BF16 = ml_dtypes.bfloat16


def bf(x):
    return np.asarray(x, np.float32).astype(BF16)


def f64(x):
    return np.asarray(x).astype(np.float64)

def planes(Y):
    n, m = Y.shape
    b = f64(bf(Y)).reshape(n // 32, 32, m)
    amax = np.abs(b).max(1)
    byte = np.clip(np.where(amax > 0, np.frexp(amax)[1] - 1 + 127 - 7, 1), 1, 254)
    codes = (b * np.exp2(127.0 - byte)[:, None, :]).reshape(n, m).astype(np.float32).astype(ml_dtypes.float8_e4m3fn).view(np.uint8)
    words = codes.reshape(n // 512, 128, 4, m).transpose(0, 1, 3, 2)
    return np.ascontiguousarray(words), np.ascontiguousarray(byte.astype(np.uint8).reshape(n // 512, 16, m))


B, T, D, F, S = 2, 1024, 512, 1536, 512

GELU_C = np.sqrt(2.0 / np.pi)

def gelu(a):
    return 0.5 * a * (1.0 + np.tanh(GELU_C * (a + 0.044715 * a ** 3)))

def setup_inputs():
    s = mx_kscale(D)
    t = mx_kscale(T)
    returns = np.random.randn(B, T, D) * s
    w_in = np.random.randn(D, F) / np.sqrt(D) / s[:, None]
    time_gain = np.exp(0.3 * np.random.randn(T)) * t
    w_time = 1.5 * np.random.randn(T, S) / np.sqrt(T) / t[:, None]
    pos = 0.5 * np.random.randn(S, F)
    feat_gain = np.exp(0.8 * np.random.randn(F))
    return {"returns": bf(returns), "w_in": bf(w_in), "time_gain": bf(time_gain),
            "w_time": bf(w_time), "pos": bf(pos), "feat_gain": bf(feat_gain)}

def reference(returns, w_in, time_gain, w_time, pos, feat_gain):
    R = f64(returns).reshape(B * T, D)
    A = mxq(R, 1, "e4m3") @ mxq(f64(w_in), 0, "e4m3")
    H = gelu(A).reshape(B, T, F) * f64(time_gain)[:, None]
    Ht = H.transpose(1, 0, 2).reshape(T, B * F)
    Z = mxq(f64(w_time), 0, "e4m3").T @ mxq(Ht, 0, "e4m3")
    Z = Z.reshape(S, B, F).transpose(1, 0, 2)
    y = (Z + f64(pos)) * f64(feat_gain)
    Y = y.reshape(B * S, F).T
    words, scales = planes(Y)
    return y, words, scales

@@ -1,0 +1,473 @@
+from contextlib import ExitStack
+
+import concourse.mybir as mybir
+from concourse.masks import make_identity
+
+B, T, D, F, S = 2, 1024, 512, 1536, 512
+FLOPS = 2 * B * T * D * F + 2 * B * S * T * F
+
+F32 = mybir.dt.float32
+BF16 = mybir.dt.bfloat16
+U32 = mybir.dt.uint32
+I32 = mybir.dt.int32
+U8 = mybir.dt.uint8
+FP8X4 = mybir.dt.float8_e4m3fn_x4
+ACT = mybir.ActivationFunctionType
+ALU = mybir.AluOpType
+
+P = 128
+PACK = 4
+GROUP = P * PACK
+HALF = GROUP // 2
+NG = F // GROUP
+NI = T // GROUP
+UNITS = [(b, g) for g in range(NG) for b in range(B)]
+LAST = len(UNITS) - 1
+SCALAR_BANKS = 6
+
+
+def halves(h):
+    return slice(h * HALF, (h + 1) * HALF)
+
+
+def pieces(n):
+    return [halves(0), halves(1)] if n == LAST else [slice(0, S)]
+
+
+def engine_orders():
+    tensor, scalar, vector, gpsimd, sync = [], [], [], [], []
+
+    def to_scalar(turn, read, *args):
+        tensor.append((turn,) + args)
+        scalar.append((read,) + args)
+
+    def gelus(n, steps):
+        for s in steps:
+            to_scalar("first", "gelu", n, s)
+
+    def r_pair(b, i):
+        for tp in range(2):
+            to_scalar("r_turn", "r_copy", b, i, tp)
+
+    def y_out(n, chunks):
+        for c in chunks:
+            to_scalar("y_turn", "y_copy", n, c)
+            if c % 2 == 1:
+                sync.append(("store_rows", n, c - 1, 2))
+
+    r_pair(0, 0)
+    gelus(0, [0, 1])
+    r_pair(0, 1)
+    gelus(0, [2, 3, 4, 5])
+    scalar.append(("wt_group", 0, 1))
+    gelus(0, [6, 7])
+    r_pair(1, 0)
+    scalar.append(("wt_group", 1, 1))
+    to_scalar("pos_turn", "pos_scale", 0, 0)
+    gelus(1, [0, 1])
+    to_scalar("pos_turn", "pos_scale", 0, 1)
+    r_pair(1, 1)
+    vector.extend([("w_group", 0, 0), ("r_quant", 0, 0, 0), ("w_quant", 0, 0), ("w_group", 0, 1), ("r_quant", 0, 0, 1)])
+    vector.extend([("w_quant", 0, 1), ("fgain_cast",), ("scale_time", 0, 0), ("r_quant", 0, 1, 0), ("r_quant", 0, 1, 1)])
+    vector.extend([("wt_group", 0, 0), ("scale_time", 0, 1), ("scale_time", 0, 2), ("h_quant", 0, 0), ("wt_quant", 0)])
+    vector.extend([("r_quant", 1, 0, 0), ("r_quant", 1, 0, 1), ("wt_group", 1, 0), ("scale_time", 0, 3)])
+    vector.extend([("wt_quant", 1), ("h_quant", 0, 1)])
+
+    for n in range(1, LAST + 1):
+        prev = n - 1
+        g = UNITS[n][1]
+        gelus(n, [2, 3])
+        tensor.extend([("second", prev, 0, 0), ("second", prev, 1, 0)])
+        if n > 1:
+            gelus(n, [4, 5])
+        tensor.extend([("second", prev, 2, 0), ("second", prev, 3, 0)])
+        if n == 1:
+            gelus(n, [4, 5])
+        gelus(n, [6, 7])
+        if n in (1, 3):
+            scalar.extend([("w_group", g + 1, 0), ("w_group", g + 1, 1)])
+        if n in (2, 4):
+            to_scalar("pos_turn", "pos_scale", g, 0)
+            to_scalar("pos_turn", "pos_scale", g, 1)
+        y_out(prev, [0, 1])
+        if n < LAST:
+            gelus(n + 1, [0, 1])
+        y_out(prev, [2, 3])
+        if n == LAST:
+            scalar.append(("y_group", prev, 1))
+        vector.append(("scale_time", n, 0))
+        if n == 1:
+            vector.extend([("r_quant", 1, 1, 0), ("r_quant", 1, 1, 1)])
+        vector.extend([("finish", prev, 0, 0), ("finish", prev, 1, 0), ("scale_time", n, 1)])
+        vector.extend([("finish", prev, 2, 0), ("finish", prev, 3, 0), ("h_quant", n, 0), ("scale_time", n, 2)])
+        if n in (1, 3):
+            vector.append(("w_quant", g + 1, 0))
+        vector.append(("y_group", prev, 0))
+        if n < LAST:
+            vector.append(("y_group", prev, 1))
+        if n in (1, 3):
+            vector.append(("w_quant", g + 1, 1))
+        if n < LAST:
+            vector.extend([("scale_time", n, 3), ("y_quant", prev, 0), ("h_quant", n, 1)])
+            sync.append(("store_words", prev))
+        if prev % 2 == 1:
+            sync.append(("store_scales", prev // 2))
+
+    vector.remove(("y_group", LAST - 1, 0))
+    vector.extend([("scale_time", LAST, 3), ("y_group", LAST - 1, 0), ("h_quant", LAST, 1), ("y_quant", LAST - 1, 0)])
+    sync.append(("store_words", LAST - 1))
+    for k in range(2):
+        for e in range(PACK):
+            tensor.append(("second", LAST, e, k))
+            vector.append(("finish", LAST, e, k))
+    scalar.append(("y_group", LAST, 0))
+    y_out(LAST, [0, 1, 2])
+    tensor.append(("y_turn", LAST, 3))
+    vector.extend([("y_group", LAST, 1), ("y_quant", LAST, 0), ("y_copy", LAST, 3), ("y_quant", LAST, 1)])
+    sync.extend([("store_rows", LAST, 2, 1), ("store_rows", LAST, 3, 1), ("store_words", LAST), ("store_scales", NG - 1)])
+    return {"tensor": tensor, "scalar": scalar, "vector": vector, "gpsimd": gpsimd, "sync": sync}
+
+
+def needs(step):
+    name, args = step[0], step[1:]
+    if name == "first":
+        (b, g), s = UNITS[args[0]], args[1]
+        return [("r_quant", b, s // 4, s % 2), ("w_quant", g, (s // 2) % 2)]
+    if name == "gelu":
+        return [("first",) + args]
+    if name == "scale_time":
+        return [("gelu", args[0], 2 * args[1]), ("gelu", args[0], 2 * args[1] + 1)]
+    if name == "h_quant":
+        return [("scale_time", args[0], 2 * args[1]), ("scale_time", args[0], 2 * args[1] + 1)]
+    if name == "second":
+        return [("h_quant", args[0], i) for i in range(NI)] + [("wt_quant", i) for i in range(NI)]
+    if name == "finish":
+        return [("second",) + args, ("pos_scale", UNITS[args[0]][1], args[1] // 2)]
+    if name == "y_turn":
+        return [("finish", args[0], e, args[1] * len(pieces(args[0])) // PACK) for e in range(PACK)]
+    if name == "y_group":
+        return [("finish", args[0], e, args[1] * len(pieces(args[0])) // 2) for e in range(PACK)]
+    if name == "y_quant":
+        return [("y_group", args[0], args[1])] if args[0] == LAST else [("y_group", args[0], h) for h in range(2)]
+    if name == "store_scales":
+        return [("y_quant", n, len(pieces(n)) - 1) for n in range(LAST + 1) if UNITS[n][1] == args[0]]
+    if name == "store_rows":
+        return [("y_copy", args[0], args[1] + c) for c in range(args[2])]
+    if name == "store_words":
+        return [("y_quant", args[0], len(pieces(args[0])) - 1)]
+    if name == "wt_quant":
+        return [("wt_group", args[0], h) for h in range(2)]
+    if name == "pos_scale":
+        return [("pos_turn",) + args, ("fgain_cast",)]
+    before = {
+        "r_copy": "r_turn",
+        "r_quant": "r_copy",
+        "w_quant": "w_group",
+        "y_copy": "y_turn",
+    }
+    return [(before[name],) + args] if name in before else []
+
+
+def tile_return_time_projection_h3_kernel(
+    tc, returns, w_in, time_gain, w_time, pos, feat_gain, out_0, out_1, out_2
+):
+    nc = tc.nc
+    with ExitStack() as ctx:
+        keep = ctx.enter_context(tc.tile_pool(name="keep", bufs=1))
+        work = ctx.enter_context(tc.tile_pool(name="work", bufs=2))
+        psum = ctx.enter_context(tc.psum_pool(name="psum", bufs=1))
+        ctx.enter_context(tc.manual_schedule())
+
+        ident = keep.tile([P, P], F32, name="ident")
+        warm = keep.tile([P, 8], F32, name="warm")
+        gain = keep.tile([P, NI, PACK], BF16, name="gain")
+        fgain_raw = keep.tile([P, NG, PACK], BF16, name="fgain_raw")
+        fgain = keep.tile([P, NG, PACK], F32, name="fgain")
+        r_raw = keep.tile([P, B, NI, PACK, D], BF16, name="r_raw")
+        w_raw = keep.tile([P, NG, PACK, GROUP], BF16, name="w_raw")
+        wt_raw = keep.tile([P, NI, PACK, S], BF16, name="wt_raw")
+        pos_raw = keep.tile([P, NG, PACK, GROUP], BF16, name="pos_raw")
+        r_codes = keep.tile([P, B, NI, GROUP], U32, name="r_codes", align_bytes=64)
+        r_scales = keep.tile([P, B, NI, GROUP], U8, name="r_scales", align_bytes=64)
+        w_codes = keep.tile([P, NG, GROUP], U32, name="w_codes", align_bytes=64)
+        w_scales = keep.tile([P, NG, GROUP], U8, name="w_scales", align_bytes=64)
+        wt_codes = keep.tile([P, NI, S], U32, name="wt_codes", align_bytes=64)
+        wt_scales = keep.tile([P, NI, S], U8, name="wt_scales", align_bytes=64)
+        pos_gain = keep.tile([P, NG, PACK, S], F32, name="pos_gain")
+        y_codes = keep.tile([P, NG, B, S], U32, name="y_codes", align_bytes=64)
+        y_scales = keep.tile([P, NG, B, S], U8, name="y_scales", align_bytes=64)
+
+        live = {}
+
+        def shared(key, shape, dtype, bufs):
+            if key not in live:
+                live[key] = work.tile(shape, dtype, name=key[0], bufs=bufs, align_bytes=64)
+            return live[key]
+
+        def scalar_bank(key, shape):
+            live[key] = psum.tile(shape, F32, name="scalar_bank", bufs=SCALAR_BANKS)
+            return live[key]
+
+        def quantize(codes, scales, grouped):
+            nc.vector.quantize_mx(out=codes.bitcast(FP8X4), scales=scales, in_=grouped)
+
+        def interleave(engine, dst, src):
+            dst_v = dst.rearrange("p (c i) t -> p c t i", i=PACK)
+            src_v = src.rearrange("p t (c i) -> p c t i", i=PACK)
+            if engine == "scalar":
+                nc.scalar.copy(out=dst_v, in_=src_v)
+            elif engine == "gpsimd":
+                nc.gpsimd.tensor_scalar(out=dst_v, in0=src_v, scalar1=1.0, scalar2=1.0, op0=ALU.mult, op1=ALU.mult)
+            else:
+                nc.vector.tensor_copy(out=dst_v, in_=src_v)
+
+        def copy(engine, dst, src):
+            if engine == "scalar":
+                nc.scalar.copy(out=dst, in_=src)
+            else:
+                nc.vector.tensor_copy(out=dst, in_=src)
+
+        def load_r(b, i, tp):
+            rows = returns[b, i * GROUP : (i + 1) * GROUP, :].rearrange("(p t) d -> p t d", t=PACK)
+            nc.sync.dma_start(out=r_raw[:, b, i, tp, :], in_=rows[:, tp, :])
+
+        def load_w(g, cols):
+            rows = w_in[:, g * GROUP : (g + 1) * GROUP].rearrange("(p t) f -> p t f", t=PACK)
+            nc.sync.dma_start(out=w_raw[:, g, :, cols], in_=rows[:, :, cols])
+
+        def load_wt(i):
+            rows = w_time[i * GROUP : (i + 1) * GROUP, :].rearrange("(p t) s -> p t s", t=PACK)
+            nc.sync.dma_start(out=wt_raw[:, i, :, :], in_=rows)
+
+        def load_pos(g):
+            rows = pos[:, g * GROUP : (g + 1) * GROUP].rearrange("(c p) f -> p c f", p=P)
+            nc.sync.dma_start(out=pos_raw[:, g, :, :], in_=rows)
+
+        def fgain_cast(engine):
+            copy(engine, fgain[:], fgain_raw[:])
+
+
+        def r_turn(engine, b, i, tp):
+            bank = scalar_bank(("r_bank", b, i, tp), [P, 2, 2, P])
+            for t in range(2):
+                words = r_raw[:, b, i, 2 * tp + t, :].bitcast(F32)
+                for u in range(2):
+                    nc.tensor.transpose(bank[:, t, u, :], words[:, u : D // 2 : 2], ident[:])
+
+        def r_copy(engine, b, i, tp):
+            grouped = shared(("r_grouped", b, i, tp), [P, 2 * P * PACK], BF16, 3)
+            copy(
+                engine,
+                grouped[:].bitcast(F32).rearrange("p (t r u) -> p t r u", t=2, u=2),
+                live["r_bank", b, i, tp][:].rearrange("p t u r -> p t r u"),
+            )
+
+        def r_quant(engine, b, i, tp):
+            quantize(r_codes[:, b, i, halves(tp)], r_scales[:, b, i, halves(tp)], live["r_grouped", b, i, tp][:])
+
+        def w_group(engine, g, h):
+            grouped = shared(("w_grouped", g, h), [P, HALF, PACK], BF16, 2)
+            interleave(engine, grouped[:], w_raw[:, g, :, halves(h)])
+
+        def w_quant(engine, g, h):
+            grouped = live["w_grouped", g, h][:].rearrange("p c t -> p (c t)")
+            quantize(w_codes[:, g, halves(h)], w_scales[:, g, halves(h)], grouped)
+
+        def wt_group(engine, i, h):
+            grouped = shared(("wt_grouped", i), [P, S, PACK], BF16, 2)
+            interleave(engine, grouped[:, halves(h), :], wt_raw[:, i, :, halves(h)])
+
+        def wt_quant(engine, i):
+            quantize(wt_codes[:, i, :], wt_scales[:, i, :], live["wt_grouped", i][:].rearrange("p c t -> p (c t)"))
+
+        def pos_turn(engine, g, u):
+            bank = scalar_bank(("pos_bank", g, u), [P, PACK, P])
+            for c in range(PACK):
+                words = pos_raw[:, g, c, :].bitcast(F32)
+                nc.tensor.transpose(bank[:, c, :], words[:, u : GROUP // 2 : 2], ident[:])
+
+        def pos_scale(engine, g, u):
+            pairs = live["pos_bank", g, u][:].rearrange("p c r -> p (c r)").bitcast(BF16)
+            for e in range(2):
+                t = 2 * u + e
+                nc.scalar.activation(
+                    out=pos_gain[:, g, t, :], in_=pairs[:, e : 2 * S : 2], func=ACT.Copy, scale=fgain[:, g, t : t + 1]
+                )
+
+        def first(engine, n, s):
+            b, g = UNITS[n]
+            i, h, tp = s // 4, (s // 2) % 2, s % 2
+            bank = scalar_bank(("first_bank", n, s), [P, 2, HALF])
+            for t in range(2):
+                rows = slice((2 * tp + t) * P, (2 * tp + t + 1) * P)
+                nc.tensor.matmul_mx(
+                    out=bank[:, t, :],
+                    lhsT=r_codes[:, b, i, rows].bitcast(FP8X4),
+                    lhsT_scale=r_scales[:, b, i, rows],
+                    rhs=w_codes[:, g, halves(h)].bitcast(FP8X4),
+                    rhs_scale=w_scales[:, g, halves(h)],
+                    start=True,
+                    stop=True,
+                )
+
+        def gelu(engine, n, s):
+            act = shared(("act", n, s // 2), [P, 2, HALF, 2], F32, 5)
+            nc.scalar.activation(
+                out=act[:, s % 2, :, :].rearrange("p (e m) t -> p e m t", e=PACK),
+                in_=live["first_bank", n, s][:].rearrange("p t (m e) -> p e m t", e=PACK),
+                func=ACT.Gelu_apprx_tanh,
+            )
+
+        def scale_time(engine, n, q):
+            i, h = q // 2, q % 2
+            grouped = shared(("h_grouped", n, i), [P, PACK, P, PACK], BF16, 3)
+            m = P // 2
+            if engine == "gpsimd":
+                gain_v = gain[:, i, :].rearrange("p (a t) -> p a t", a=2)
+                multiply = nc.gpsimd.tensor_tensor
+            else:
+                gain_v = gain[:, i, :].rearrange("p (a t) -> p a t", a=2)
+                multiply = nc.vector.tensor_tensor
+            multiply(
+                out=grouped[:, :, h * m : (h + 1) * m, :].rearrange("p e m (a t) -> p e m a t", a=2),
+                in0=live["act", n, q][:].rearrange("p a (e m) t -> p e m a t", e=PACK),
+                in1=gain_v.unsqueeze(1).unsqueeze(1).to_broadcast([P, PACK, m, 2, 2]),
+                op=ALU.mult,
+            )
+
+        def h_quant(engine, n, i):
+            codes = shared(("h_codes", n, i), [P, GROUP], U32, 4)
+            scales = shared(("h_scales", n, i), [P, GROUP], U8, 4)
+            quantize(codes[:], scales[:], live["h_grouped", n, i][:].rearrange("p e m t -> p (e m t)"))
+
+        def second(engine, n, e, k):
+            cols = pieces(n)[k]
+            if n == LAST and e >= 2:
+                bank = scalar_bank(("second_bank", n, e, k), [P, HALF])
+            else:
+                bank = psum.tile([P, cols.stop - cols.start], F32, name="second_bank", bufs=2)
+            rows = slice(e * P, (e + 1) * P)
+            for i in range(NI):
+                nc.tensor.matmul_mx(
+                    out=bank[:],
+                    lhsT=live["h_codes", n, i][:, rows].bitcast(FP8X4),
+                    lhsT_scale=live["h_scales", n, i][:, rows],
+                    rhs=wt_codes[:, i, cols].bitcast(FP8X4),
+                    rhs_scale=wt_scales[:, i, cols],
+                    start=(i == 0),
+                    stop=(i == NI - 1),
+                )
+            live["second_bank", n, e, k] = bank
+
+        def finish(engine, n, e, k):
+            g = UNITS[n][1]
+            cols = pieces(n)[k]
+            turned = shared(("y_turned", n), [P, PACK, S], F32, 3)
+            nc.vector.scalar_tensor_tensor(
+                out=turned[:, e, cols],
+                in0=live["second_bank", n, e, k][:],
+                scalar=fgain[:, g, e : e + 1],
+                in1=pos_gain[:, g, e, cols],
+                op0=ALU.mult,
+                op1=ALU.add,
+            )
+
+        def y_turn(engine, n, c):
+            bank = scalar_bank(("y_bank", n, c), [P, PACK, P])
+            for e in range(PACK):
+                nc.tensor.transpose(bank[:, e, :], live["y_turned", n][:, e, c * P : (c + 1) * P], ident[:])
+
+        def y_copy(engine, n, c):
+            rows = shared(("y_rows", n, c // 2), [P, 2, P, PACK], F32, 3)
+            copy(engine, rows[:, c % 2, :, :], live["y_bank", n, c][:].rearrange("p e m -> p m e"))
+
+        def store_rows(engine, n, c, count):
+            b, g = UNITS[n]
+            rows = out_0[b, c * P : (c + count) * P, g * GROUP : (g + 1) * GROUP]
+            nc.sync.dma_start(
+                out=rows.rearrange("(c p) f -> p c f", p=P),
+                in_=live["y_rows", n, c // 2][:, c % 2 : c % 2 + count, :, :].rearrange("p c m e -> p c (m e)"),
+            )
+
+        def y_group(engine, n, h):
+            grouped = shared(("y_grouped", n), [P, S, PACK], BF16, 2)
+            interleave(engine, grouped[:, halves(h), :], live["y_turned", n][:, :, halves(h)])
+
+        def y_quant(engine, n, k):
+            b, g = UNITS[n]
+            cols = pieces(n)[k]
+            grouped = live["y_grouped", n][:, cols, :].rearrange("p c t -> p (c t)")
+            quantize(y_codes[:, g, b, cols], y_scales[:, g, b, cols], grouped)
+
+        def store_words(engine, n):
+            b, g = UNITS[n]
+            words = out_1[g].rearrange("p m t -> p (m t)").bitcast(I32)
+            nc.sync.dma_start(out=words[:, b * S : (b + 1) * S], in_=y_codes[:, g, b, :].bitcast(I32))
+
+        def store_scales(engine, g):
+            rows = out_2[g].bitcast(I32)
+            for q in range(4):
+                nc.sync.dma_start(
+                    out=rows[4 * q : 4 * q + 4, :],
+                    in_=y_scales[32 * q : 32 * q + 4, g, :, :].rearrange("p b s -> p (b s)").bitcast(I32),
+                )
+
+        lo, hi, whole = slice(0, 2), slice(2, 4), slice(0, 4)
+        load_r(0, 0, lo)
+        load_w(0, halves(0))
+        load_r(0, 0, hi)
+        load_w(0, halves(1))
+        nc.sync.dma_start(out=gain[:], in_=time_gain.rearrange("(i p t) -> p i t", p=P, t=PACK))
+        load_r(0, 1, whole)
+        nc.sync.dma_start(out=fgain_raw[:], in_=feat_gain.rearrange("(g p t) -> p g t", p=P, t=PACK))
+        load_wt(0)
+        load_r(1, 0, whole)
+        load_wt(1)
+        load_pos(0)
+        load_r(1, 1, whole)
+        load_w(1, slice(0, GROUP))
+        load_pos(1)
+        load_w(2, slice(0, GROUP))
+        load_pos(2)
+
+        make_identity(nc, ident[:])
+        nc.vector.memset(warm[:], 0.0)
+        nc.scalar.activation(out=warm[:, 0:1], in_=warm[:, 1:2], func=ACT.Gelu_apprx_tanh)
+
+        emit = {
+            "fgain_cast": fgain_cast,
+            "r_turn": r_turn,
+            "r_copy": r_copy,
+            "r_quant": r_quant,
+            "w_group": w_group,
+            "w_quant": w_quant,
+            "wt_group": wt_group,
+            "wt_quant": wt_quant,
+            "pos_turn": pos_turn,
+            "pos_scale": pos_scale,
+            "first": first,
+            "gelu": gelu,
+            "scale_time": scale_time,
+            "h_quant": h_quant,
+            "second": second,
+            "finish": finish,
+            "y_turn": y_turn,
+            "y_copy": y_copy,
+            "store_rows": store_rows,
+            "y_group": y_group,
+            "y_quant": y_quant,
+            "store_words": store_words,
+            "store_scales": store_scales,
+        }
+        queues = engine_orders()
+        written = set()
+        while any(queues.values()):
+            moved = False
+            for engine, queue in queues.items():
+                while queue and all(need in written for need in needs(queue[0])):
+                    step = queue[0]
+                    queue.remove(step)
+                    emit[step[0]](engine, *step[1:])
+                    written.add(step)
+                    moved = True
+            assert moved

@@ -23,7 +23,7 @@ NG = F // GROUP
 NI = T // GROUP
 UNITS = [(b, g) for g in range(NG) for b in range(B)]
 LAST = len(UNITS) - 1
-SCALAR_BANKS = 6
+SCALAR_BANKS = 5
 
 
 def halves(h):
@@ -56,75 +56,67 @@ def engine_orders():
                 sync.append(("store_rows", n, c - 1, 2))
 
     r_pair(0, 0)
+    tensor.append(("gain_turn",))
     gelus(0, [0, 1])
     r_pair(0, 1)
-    gelus(0, [2, 3, 4, 5])
-    scalar.append(("wt_group", 0, 1))
-    gelus(0, [6, 7])
+    gelus(0, [2, 3, 4, 5, 6, 7])
     r_pair(1, 0)
     scalar.append(("wt_group", 1, 1))
-    to_scalar("pos_turn", "pos_scale", 0, 0)
-    gelus(1, [0, 1])
-    to_scalar("pos_turn", "pos_scale", 0, 1)
     r_pair(1, 1)
+    gelus(1, [0, 1])
+    to_scalar("pos_turn", "pos_scale", 0, 0)
+    gelus(1, [2, 3])
+    to_scalar("pos_turn", "pos_scale", 0, 1)
     vector.extend([("w_group", 0, 0), ("r_quant", 0, 0, 0), ("w_quant", 0, 0), ("w_group", 0, 1), ("r_quant", 0, 0, 1)])
-    vector.extend([("w_quant", 0, 1), ("fgain_cast",), ("scale_time", 0, 0), ("r_quant", 0, 1, 0), ("r_quant", 0, 1, 1)])
-    vector.extend([("wt_group", 0, 0), ("scale_time", 0, 1), ("scale_time", 0, 2), ("h_quant", 0, 0), ("wt_quant", 0)])
-    vector.extend([("r_quant", 1, 0, 0), ("r_quant", 1, 0, 1), ("wt_group", 1, 0), ("scale_time", 0, 3)])
-    vector.extend([("wt_quant", 1), ("h_quant", 0, 1)])
+    vector.extend([("w_quant", 0, 1), ("scale_time", 0, 0), ("r_quant", 0, 1, 0), ("r_quant", 0, 1, 1)])
+    vector.extend([("wt_group", 0, 0), ("wt_group", 0, 1), ("wt_quant", 0), ("scale_time", 0, 1)])
+    vector.extend([("scale_time", 0, 2), ("scale_time", 0, 3), ("r_quant", 1, 0, 0), ("r_quant", 1, 0, 1), ("fgain_cast",), ("h_quant", 0, 0)])
+    vector.extend([("wt_group", 1, 0), ("h_quant", 0, 1), ("wt_quant", 1)])
+    vector.extend([("w_quant", 1, 0), ("r_quant", 1, 1, 0), ("w_quant", 1, 1), ("r_quant", 1, 1, 1)])
+    gpsimd.extend([("w_group", 1, 0), ("w_group", 1, 1), ("w_group", 2, 0), ("w_group", 2, 1), ("scale_time", 1, 2)])
 
     for n in range(1, LAST + 1):
         prev = n - 1
         g = UNITS[n][1]
-        gelus(n, [2, 3])
+        gelus(n, [4, 5])
         tensor.extend([("second", prev, 0, 0), ("second", prev, 1, 0)])
-        if n > 1:
-            gelus(n, [4, 5])
-        tensor.extend([("second", prev, 2, 0), ("second", prev, 3, 0)])
-        if n == 1:
-            gelus(n, [4, 5])
         gelus(n, [6, 7])
-        if n in (1, 3):
-            scalar.extend([("w_group", g + 1, 0), ("w_group", g + 1, 1)])
-        if n in (2, 4):
-            to_scalar("pos_turn", "pos_scale", g, 0)
-            to_scalar("pos_turn", "pos_scale", g, 1)
-        y_out(prev, [0, 1])
         if n < LAST:
-            gelus(n + 1, [0, 1])
-        y_out(prev, [2, 3])
-        if n == LAST:
-            scalar.append(("y_group", prev, 1))
+            gelus(n + 1, [0])
+        tensor.extend([("second", prev, 2, 0), ("second", prev, 3, 0)])
+        if n < LAST:
+            gelus(n + 1, [1])
+        if n in (1, 2, 3, 4):
+            to_scalar("pos_turn", "pos_scale", (n + 1) // 2, (n + 1) % 2)
+        y_out(prev, [0, 1, 2, 3])
+        if n < LAST:
+            gelus(n + 1, [2, 3])
         vector.append(("scale_time", n, 0))
-        if n == 1:
-            vector.extend([("r_quant", 1, 1, 0), ("r_quant", 1, 1, 1)])
         vector.extend([("finish", prev, 0, 0), ("finish", prev, 1, 0), ("scale_time", n, 1)])
-        vector.extend([("finish", prev, 2, 0), ("finish", prev, 3, 0), ("h_quant", n, 0), ("scale_time", n, 2)])
-        if n in (1, 3):
-            vector.append(("w_quant", g + 1, 0))
-        vector.append(("y_group", prev, 0))
-        if n < LAST:
-            vector.append(("y_group", prev, 1))
-        if n in (1, 3):
-            vector.append(("w_quant", g + 1, 1))
-        if n < LAST:
-            vector.extend([("scale_time", n, 3), ("y_quant", prev, 0), ("h_quant", n, 1)])
-            sync.append(("store_words", prev))
-        if prev % 2 == 1:
-            sync.append(("store_scales", prev // 2))
+        vector.extend([("finish", prev, 2, 0), ("finish", prev, 3, 0)])
+        vector.extend([("scale_time", n, 3), ("h_quant", n, 0), ("h_quant", n, 1)])
+        if n == 1:
+            vector.extend([("w_quant", 2, 0), ("w_quant", 2, 1)])
+        else:
+            gpsimd.extend([("y_group", n - 2, 0), ("y_group", n - 2, 1), ("scale_time", n, 2)])
+            vector.append(("y_quant", n - 2, 0))
+            sync.append(("store_words", n - 2))
+        if n == 3:
+            sync.append(("store_scales", 0))
+        if n == LAST:
+            sync.append(("store_scales", 1))
 
-    vector.remove(("y_group", LAST - 1, 0))
-    vector.extend([("scale_time", LAST, 3), ("y_group", LAST - 1, 0), ("h_quant", LAST, 1), ("y_quant", LAST - 1, 0)])
-    sync.append(("store_words", LAST - 1))
+    gpsimd.append(("y_group", LAST - 1, 0))
+    scalar.append(("y_group", LAST - 1, 1))
     for k in range(2):
         for e in range(PACK):
             tensor.append(("second", LAST, e, k))
             vector.append(("finish", LAST, e, k))
-    scalar.append(("y_group", LAST, 0))
-    y_out(LAST, [0, 1, 2])
-    tensor.append(("y_turn", LAST, 3))
-    vector.extend([("y_group", LAST, 1), ("y_quant", LAST, 0), ("y_copy", LAST, 3), ("y_quant", LAST, 1)])
-    sync.extend([("store_rows", LAST, 2, 1), ("store_rows", LAST, 3, 1), ("store_words", LAST), ("store_scales", NG - 1)])
+    for c in range(PACK):
+        to_scalar("y_turn", "y_copy", LAST, c)
+        sync.append(("store_rows", LAST, c, 1))
+    vector.extend([("y_quant", LAST - 1, 0), ("y_group", LAST, 0), ("y_group", LAST, 1), ("y_quant", LAST, 0), ("y_quant", LAST, 1)])
+    sync.extend([("store_words", LAST - 1), ("store_words", LAST), ("store_scales", NG - 1)])
     return {"tensor": tensor, "scalar": scalar, "vector": vector, "gpsimd": gpsimd, "sync": sync}
 
 
@@ -136,7 +128,7 @@ def needs(step):
     if name == "gelu":
         return [("first",) + args]
     if name == "scale_time":
-        return [("gelu", args[0], 2 * args[1]), ("gelu", args[0], 2 * args[1] + 1)]
+        return [("gelu", args[0], 2 * args[1]), ("gelu", args[0], 2 * args[1] + 1), ("gain_turn",)]
     if name == "h_quant":
         return [("scale_time", args[0], 2 * args[1]), ("scale_time", args[0], 2 * args[1] + 1)]
     if name == "second":
@@ -146,7 +138,12 @@ def needs(step):
     if name == "y_turn":
         return [("finish", args[0], e, args[1] * len(pieces(args[0])) // PACK) for e in range(PACK)]
     if name == "y_group":
-        return [("finish", args[0], e, args[1] * len(pieces(args[0])) // 2) for e in range(PACK)]
+        freed = [("w_quant", NG - 1, 1)] if args[0] == 0 else [("y_quant", args[0] - 1, 0)] if args[0] < LAST else []
+        return freed + [("finish", args[0], e, args[1] * len(pieces(args[0])) // 2) for e in range(PACK)]
+    if name == "w_group":
+        return [[], [("wt_quant", 0)], [("w_quant", 1, 1)]][args[0]]
+    if name == "wt_group":
+        return [("w_quant", 0, 1)]
     if name == "y_quant":
         return [("y_group", args[0], args[1])] if args[0] == LAST else [("y_group", args[0], h) for h in range(2)]
     if name == "store_scales":
@@ -196,12 +193,13 @@ def tile_return_time_projection_h3_kernel(
         pos_gain = keep.tile([P, NG, PACK, S], F32, name="pos_gain")
         y_codes = keep.tile([P, NG, B, S], U32, name="y_codes", align_bytes=64)
         y_scales = keep.tile([P, NG, B, S], U8, name="y_scales", align_bytes=64)
-
+        gain_rows = keep.tile([P, GROUP], BF16, name="gain_rows")
+        gain_bank = psum.tile([P, P], F32, name="gain_bank")
         live = {}
 
-        def shared(key, shape, dtype, bufs):
+        def shared(key, shape, dtype, bufs, tag=None):
             if key not in live:
-                live[key] = work.tile(shape, dtype, name=key[0], bufs=bufs, align_bytes=64)
+                live[key] = work.tile(shape, dtype, name=key[0], tag=tag or key[0], bufs=bufs, align_bytes=64)
             return live[key]
 
         def scalar_bank(key, shape):
@@ -246,6 +244,8 @@ def tile_return_time_projection_h3_kernel(
         def fgain_cast(engine):
             copy(engine, fgain[:], fgain_raw[:])
 
+        def gain_turn(engine):
+            nc.tensor.transpose(gain_bank[:], gain_rows[:].bitcast(F32)[:, 0 : GROUP // 2 : 2], ident[:])
 
         def r_turn(engine, b, i, tp):
             bank = scalar_bank(("r_bank", b, i, tp), [P, 2, 2, P])
@@ -266,15 +266,16 @@ def tile_return_time_projection_h3_kernel(
             quantize(r_codes[:, b, i, halves(tp)], r_scales[:, b, i, halves(tp)], live["r_grouped", b, i, tp][:])
 
         def w_group(engine, g, h):
-            grouped = shared(("w_grouped", g, h), [P, HALF, PACK], BF16, 2)
-            interleave(engine, grouped[:], w_raw[:, g, :, halves(h)])
+            tag = "gpsimd_grouped" if engine == "gpsimd" else "vector_grouped"
+            grouped = shared(("w_grouped", g), [P, GROUP, PACK], BF16, 1, tag)
+            interleave(engine, grouped[:, halves(h), :], w_raw[:, g, :, halves(h)])
 
         def w_quant(engine, g, h):
-            grouped = live["w_grouped", g, h][:].rearrange("p c t -> p (c t)")
+            grouped = live["w_grouped", g][:, halves(h), :].rearrange("p c t -> p (c t)")
             quantize(w_codes[:, g, halves(h)], w_scales[:, g, halves(h)], grouped)
 
         def wt_group(engine, i, h):
-            grouped = shared(("wt_grouped", i), [P, S, PACK], BF16, 2)
+            grouped = shared(("wt_grouped", i), [P, S, PACK], BF16, 1, "gpsimd_grouped" if i == 0 else "vector_grouped")
             interleave(engine, grouped[:, halves(h), :], wt_raw[:, i, :, halves(h)])
 
         def wt_quant(engine, i):
@@ -311,7 +312,7 @@ def tile_return_time_projection_h3_kernel(
                 )
 
         def gelu(engine, n, s):
-            act = shared(("act", n, s // 2), [P, 2, HALF, 2], F32, 5)
+            act = shared(("act", n, s // 2), [P, 2, HALF, 2], F32, 6)
             nc.scalar.activation(
                 out=act[:, s % 2, :, :].rearrange("p (e m) t -> p e m t", e=PACK),
                 in_=live["first_bank", n, s][:].rearrange("p t (m e) -> p e m t", e=PACK),
@@ -326,7 +327,7 @@ def tile_return_time_projection_h3_kernel(
                 gain_v = gain[:, i, :].rearrange("p (a t) -> p a t", a=2)
                 multiply = nc.gpsimd.tensor_tensor
             else:
-                gain_v = gain[:, i, :].rearrange("p (a t) -> p a t", a=2)
+                gain_v = gain_bank[:].bitcast(BF16)[:, PACK * i : PACK * (i + 1)].rearrange("p (a t) -> p a t", a=2)
                 multiply = nc.vector.tensor_tensor
             multiply(
                 out=grouped[:, :, h * m : (h + 1) * m, :].rearrange("p e m (a t) -> p e m a t", a=2),
@@ -390,7 +391,8 @@ def tile_return_time_projection_h3_kernel(
             )
 
         def y_group(engine, n, h):
-            grouped = shared(("y_grouped", n), [P, S, PACK], BF16, 2)
+            tag = "gpsimd_grouped" if n < LAST else "vector_grouped"
+            grouped = shared(("y_grouped", n), [P, S, PACK], BF16, 1, tag)
             interleave(engine, grouped[:, halves(h), :], live["y_turned", n][:, :, halves(h)])
 
         def y_quant(engine, n, k):
@@ -413,21 +415,25 @@ def tile_return_time_projection_h3_kernel(
                 )
 
         lo, hi, whole = slice(0, 2), slice(2, 4), slice(0, 4)
+        nc.vector.memset(gain_rows[:].bitcast(I32), 0)
         load_r(0, 0, lo)
         load_w(0, halves(0))
         load_r(0, 0, hi)
         load_w(0, halves(1))
-        nc.sync.dma_start(out=gain[:], in_=time_gain.rearrange("(i p t) -> p i t", p=P, t=PACK))
+        gain_hbm = time_gain.rearrange("(i c) -> i c", i=NI)
+        nc.sync.dma_start(out=gain_rows[0 : 2 * NI : 2, :], in_=gain_hbm)
+        nc.sync.dma_start(out=gain_rows[1 : 2 * NI : 2, 0 : GROUP - 2], in_=gain_hbm[:, 2:GROUP])
         load_r(0, 1, whole)
-        nc.sync.dma_start(out=fgain_raw[:], in_=feat_gain.rearrange("(g p t) -> p g t", p=P, t=PACK))
         load_wt(0)
-        load_r(1, 0, whole)
-        load_wt(1)
-        load_pos(0)
-        load_r(1, 1, whole)
         load_w(1, slice(0, GROUP))
-        load_pos(1)
+        load_r(1, 0, whole)
+        nc.sync.dma_start(out=fgain_raw[:], in_=feat_gain.rearrange("(g p t) -> p g t", p=P, t=PACK))
+        load_wt(1)
+        load_r(1, 1, whole)
+        load_pos(0)
+        nc.sync.dma_start(out=gain[:], in_=time_gain.rearrange("(i p t) -> p i t", p=P, t=PACK))
         load_w(2, slice(0, GROUP))
+        load_pos(1)
         load_pos(2)
 
         make_identity(nc, ident[:])
@@ -436,6 +442,7 @@ def tile_return_time_projection_h3_kernel(
 
         emit = {
             "fgain_cast": fgain_cast,
+            "gain_turn": gain_turn,
             "r_turn": r_turn,
             "r_copy": r_copy,
             "r_quant": r_quant,

@@ -30,8 +30,19 @@ def halves(h):
     return slice(h * HALF, (h + 1) * HALF)
 
 
+def w_parts(g):
+    return [halves(0), halves(1)] if g == 0 else [slice(0, GROUP)]
+
+
+def y_parts(n):
+    return [halves(0), halves(1)] if n >= LAST - 1 else [slice(0, S)]
+
+
 def pieces(n):
     return [halves(0), halves(1)] if n == LAST else [slice(0, S)]
+
+
+RELAY = [("wt_grouped", 0), ("w_grouped", 1), ("w_grouped", 2)] + [("y_grouped", n) for n in range(LAST - 1)]
 
 
 def engine_orders():
@@ -43,88 +54,125 @@ def engine_orders():
 
     def gelus(n, steps):
         for s in steps:
-            to_scalar("first", "gelu", n, s)
+            if n <= LAST:
+                to_scalar("first", "gelu", n, s)
 
     def r_pair(b, i):
         for tp in range(2):
             to_scalar("r_turn", "r_copy", b, i, tp)
 
-    def y_out(n, chunks):
-        for c in chunks:
-            to_scalar("y_turn", "y_copy", n, c)
-            if c % 2 == 1:
-                sync.append(("store_rows", n, c - 1, 2))
+    def pos_pair(g, u):
+        tensor.append(("pos_turn", g, u))
+        scalar.extend([("pos_scale", g, 2 * u), ("pos_scale", g, 2 * u + 1)])
 
-    r_pair(0, 0)
+    def y_pair(n, c):
+        to_scalar("y_turn", "y_copy", n, c)
+        to_scalar("y_turn", "y_copy", n, c + 1)
+        sync.append(("store_rows", n, c, 2))
+
+    def seconds(n, groups, k):
+        tensor.extend([("second", n, e, k) for e in groups])
+
+    def finishes(n, groups, k):
+        vector.extend([("finish", n, e, k) for e in groups])
+
+    tensor.append(("r_turn", 0, 0, 0))
+    to_scalar("r_turn", "r_copy", 0, 0, 1)
     tensor.append(("gain_turn",))
+    scalar.append(("w_group", 0, 1))
     gelus(0, [0, 1])
     r_pair(0, 1)
     gelus(0, [2, 3, 4, 5, 6, 7])
     r_pair(1, 0)
+    to_scalar("r_turn", "r_copy", 1, 1, 0)
     scalar.append(("wt_group", 1, 1))
-    r_pair(1, 1)
+    to_scalar("r_turn", "r_copy", 1, 1, 1)
     gelus(1, [0, 1])
-    to_scalar("pos_turn", "pos_scale", 0, 0)
+    tensor.append(("pos_turn", 0, 0))
+    scalar.append(("pos_scale", 0, 0))
     gelus(1, [2, 3])
-    to_scalar("pos_turn", "pos_scale", 0, 1)
-    vector.extend([("w_group", 0, 0), ("r_quant", 0, 0, 0), ("w_quant", 0, 0), ("w_group", 0, 1), ("r_quant", 0, 0, 1)])
-    vector.extend([("w_quant", 0, 1), ("scale_time", 0, 0), ("r_quant", 0, 1, 0), ("r_quant", 0, 1, 1)])
-    vector.extend([("wt_group", 0, 0), ("wt_group", 0, 1), ("wt_quant", 0), ("scale_time", 0, 1)])
-    vector.extend([("scale_time", 0, 2), ("scale_time", 0, 3), ("r_quant", 1, 0, 0), ("r_quant", 1, 0, 1), ("fgain_cast",), ("h_quant", 0, 0)])
-    vector.extend([("wt_group", 1, 0), ("h_quant", 0, 1), ("wt_quant", 1)])
-    vector.extend([("w_quant", 1, 0), ("r_quant", 1, 1, 0), ("w_quant", 1, 1), ("r_quant", 1, 1, 1)])
-    gpsimd.extend([("w_group", 1, 0), ("w_group", 1, 1), ("w_group", 2, 0), ("w_group", 2, 1), ("scale_time", 1, 2)])
+    pos_pair(0, 1)
+    gelus(1, [4])
+    vector.extend([("r_copy", 0, 0, 0), ("w_group", 0, 0), ("r_quant", 0, 0, 0), ("w_quant", 0, 0), ("r_quant", 0, 0, 1)])
+    vector.extend([("w_quant", 0, 1), ("scale_time", 0, 0), ("wt_group", 0, 1), ("r_quant", 0, 1, 0), ("r_quant", 0, 1, 1)])
+    vector.extend([("wt_quant", 0), ("fgain_cast",), ("scale_time", 0, 1), ("scale_time", 0, 2), ("scale_time", 0, 3)])
+    vector.extend([("r_quant", 1, 0, 0), ("r_quant", 1, 0, 1), ("wt_group", 1, 0), ("h_quant", 0, 0), ("r_quant", 1, 1, 0)])
+    vector.extend([("h_quant", 0, 1), ("wt_quant", 1), ("w_quant", 1, 0), ("r_quant", 1, 1, 1), ("pos_scale", 0, 1)])
+    gpsimd.extend([("wt_group", 0, 0), ("w_group", 1, 0), ("w_group", 2, 0)])
 
     for n in range(1, LAST + 1):
-        prev = n - 1
-        g = UNITS[n][1]
-        gelus(n, [4, 5])
-        tensor.extend([("second", prev, 0, 0), ("second", prev, 1, 0)])
+        prev, late = n - 1, n - 2
+        seconds(prev, [0, 1], 0)
+        if n == 1:
+            gelus(n, [5])
+        elif n > 2:
+            y_pair(late, 0)
         gelus(n, [6, 7])
+        seconds(prev, [2, 3], 0)
+        if n > 1:
+            y_pair(late, 2)
+        gelus(n + 1, [0, 1])
         if n < LAST:
-            gelus(n + 1, [0])
-        tensor.extend([("second", prev, 2, 0), ("second", prev, 3, 0)])
-        if n < LAST:
-            gelus(n + 1, [1])
-        if n in (1, 2, 3, 4):
-            to_scalar("pos_turn", "pos_scale", (n + 1) // 2, (n + 1) % 2)
-        y_out(prev, [0, 1, 2, 3])
-        if n < LAST:
-            gelus(n + 1, [2, 3])
+            pos_pair((n + 1) // 2, (n + 1) % 2)
+        gelus(n + 1, [2, 3])
+        if n == 1:
+            y_pair(prev, 0)
+        gelus(n + 1, [4, 5])
         vector.append(("scale_time", n, 0))
-        vector.extend([("finish", prev, 0, 0), ("finish", prev, 1, 0), ("scale_time", n, 1)])
-        vector.extend([("finish", prev, 2, 0), ("finish", prev, 3, 0)])
+        finishes(prev, [0, 1], 0)
+        vector.append(("scale_time", n, 1))
+        finishes(prev, [2, 3], 0)
+        if n == LAST - 1:
+            scalar.remove(("y_copy", late, 3))
+            vector.append(("y_copy", late, 3))
         vector.extend([("scale_time", n, 3), ("h_quant", n, 0), ("h_quant", n, 1)])
         if n == 1:
-            vector.extend([("w_quant", 2, 0), ("w_quant", 2, 1)])
+            vector.append(("w_quant", 2, 0))
         else:
-            gpsimd.extend([("y_group", n - 2, 0), ("y_group", n - 2, 1), ("scale_time", n, 2)])
-            vector.append(("y_quant", n - 2, 0))
-            sync.append(("store_words", n - 2))
+            gpsimd.append(("y_group", late, 0))
+            vector.append(("y_quant", late, 0))
+            sync.append(("store_words", late))
+        gpsimd.append(("scale_time", n, 2))
         if n == 3:
             sync.append(("store_scales", 0))
-        if n == LAST:
-            sync.append(("store_scales", 1))
 
-    gpsimd.append(("y_group", LAST - 1, 0))
-    scalar.append(("y_group", LAST - 1, 1))
-    for k in range(2):
-        for e in range(PACK):
-            tensor.append(("second", LAST, e, k))
-            vector.append(("finish", LAST, e, k))
-    for c in range(PACK):
-        to_scalar("y_turn", "y_copy", LAST, c)
-        sync.append(("store_rows", LAST, c, 1))
-    vector.extend([("y_quant", LAST - 1, 0), ("y_group", LAST, 0), ("y_group", LAST, 1), ("y_quant", LAST, 0), ("y_quant", LAST, 1)])
-    sync.extend([("store_words", LAST - 1), ("store_words", LAST), ("store_scales", NG - 1)])
+    prev = LAST - 1
+    sync.remove(("store_words", LAST - 2))
+    y_pair(prev, 0)
+    scalar.append(("y_group", prev, 1))
+    sync.extend([("store_scales", 1), ("store_words", LAST - 2)])
+    y_pair(prev, 2)
+    tensor.remove(("y_turn", prev, 3))
+    tensor.extend([("warm", prev, 3), ("warm", prev, 3), ("y_turn", prev, 3)])
+    vector.append(("y_group", prev, 0))
+    seconds(LAST, range(PACK), 0)
+    finishes(LAST, range(PACK), 0)
+    vector.append(("y_quant", prev, 0))
+    gpsimd.append(("y_group", LAST, 0))
+    seconds(LAST, range(PACK), 1)
+    finishes(LAST, range(PACK), 1)
+    tensor.extend([("y_turn", LAST, c) for c in range(PACK)])
+    scalar.extend([("y_copy", LAST, c) for c in (0, 2, 3)])
+    vector.extend([("y_copy", LAST, 1), ("y_group", LAST, 1), ("y_quant", LAST, 0), ("y_quant", LAST, 1)])
+    sync.append(("store_words", prev))
+    sync.extend([("store_rows", LAST, c, 1) for c in range(3)])
+    sync.extend([("store_words", LAST), ("store_rows", LAST, 3, 1), ("store_scales", NG - 1)])
     return {"tensor": tensor, "scalar": scalar, "vector": vector, "gpsimd": gpsimd, "sync": sync}
+
+
+def last_read(key):
+    if key[0] == "w_grouped":
+        return [("w_quant", key[1], h) for h in range(len(w_parts(key[1])))]
+    if key[0] == "wt_grouped":
+        return [("wt_quant", key[1])]
+    return [("y_quant", key[1], k) for k in range(len(pieces(key[1])))]
 
 
 def needs(step):
     name, args = step[0], step[1:]
     if name == "first":
         (b, g), s = UNITS[args[0]], args[1]
-        return [("r_quant", b, s // 4, s % 2), ("w_quant", g, (s // 2) % 2)]
+        return [("r_quant", b, s // 4, s % 2), ("w_quant", g, (s // 2) % len(w_parts(g)))]
     if name == "gelu":
         return [("first",) + args]
     if name == "scale_time":
@@ -134,18 +182,19 @@ def needs(step):
     if name == "second":
         return [("h_quant", args[0], i) for i in range(NI)] + [("wt_quant", i) for i in range(NI)]
     if name == "finish":
-        return [("second",) + args, ("pos_scale", UNITS[args[0]][1], args[1] // 2)]
+        return [("second",) + args, ("pos_scale", UNITS[args[0]][1], args[1])]
     if name == "y_turn":
         return [("finish", args[0], e, args[1] * len(pieces(args[0])) // PACK) for e in range(PACK)]
-    if name == "y_group":
-        freed = [("w_quant", NG - 1, 1)] if args[0] == 0 else [("y_quant", args[0] - 1, 0)] if args[0] < LAST else []
+    if name in ("w_group", "wt_group", "y_group"):
+        key = (name + "ed", args[0])
+        freed = last_read(RELAY[RELAY.index(key) - 1]) if key in RELAY[1:] else []
+        if name != "y_group":
+            return freed
         return freed + [("finish", args[0], e, args[1] * len(pieces(args[0])) // 2) for e in range(PACK)]
-    if name == "w_group":
-        return [[], [("wt_quant", 0)], [("w_quant", 1, 1)]][args[0]]
-    if name == "wt_group":
-        return [("w_quant", 0, 1)]
+    if name == "warm":
+        return [("r_quant", 0, 0, 0), ("w_quant", 0, 0)]
     if name == "y_quant":
-        return [("y_group", args[0], args[1])] if args[0] == LAST else [("y_group", args[0], h) for h in range(2)]
+        return [("y_group", args[0], args[1])] if args[0] == LAST else [("y_group", args[0], h) for h in range(len(y_parts(args[0])))]
     if name == "store_scales":
         return [("y_quant", n, len(pieces(n)) - 1) for n in range(LAST + 1) if UNITS[n][1] == args[0]]
     if name == "store_rows":
@@ -155,7 +204,7 @@ def needs(step):
     if name == "wt_quant":
         return [("wt_group", args[0], h) for h in range(2)]
     if name == "pos_scale":
-        return [("pos_turn",) + args, ("fgain_cast",)]
+        return [("pos_turn", args[0], args[1] // 2), ("fgain_cast",)]
     before = {
         "r_copy": "r_turn",
         "r_quant": "r_copy",
@@ -195,6 +244,7 @@ def tile_return_time_projection_h3_kernel(
         y_scales = keep.tile([P, NG, B, S], U8, name="y_scales", align_bytes=64)
         gain_rows = keep.tile([P, GROUP], BF16, name="gain_rows")
         gain_bank = psum.tile([P, P], F32, name="gain_bank")
+        relay = keep.tile([P, GROUP, PACK], BF16, name="relay", align_bytes=64)
         live = {}
 
         def shared(key, shape, dtype, bufs, tag=None):
@@ -202,8 +252,14 @@ def tile_return_time_projection_h3_kernel(
                 live[key] = work.tile(shape, dtype, name=key[0], tag=tag or key[0], bufs=bufs, align_bytes=64)
             return live[key]
 
+        def grouped_tile(key):
+            if key in RELAY:
+                live[key] = relay
+            return shared(key, [P, GROUP, PACK], BF16, 2, "grouped")
+
         def scalar_bank(key, shape):
-            live[key] = psum.tile(shape, F32, name="scalar_bank", bufs=SCALAR_BANKS)
+            if key not in live:
+                live[key] = psum.tile(shape, F32, name="scalar_bank", bufs=SCALAR_BANKS)
             return live[key]
 
         def quantize(codes, scales, grouped):
@@ -266,16 +322,17 @@ def tile_return_time_projection_h3_kernel(
             quantize(r_codes[:, b, i, halves(tp)], r_scales[:, b, i, halves(tp)], live["r_grouped", b, i, tp][:])
 
         def w_group(engine, g, h):
-            tag = "gpsimd_grouped" if engine == "gpsimd" else "vector_grouped"
-            grouped = shared(("w_grouped", g), [P, GROUP, PACK], BF16, 1, tag)
-            interleave(engine, grouped[:, halves(h), :], w_raw[:, g, :, halves(h)])
+            grouped = grouped_tile(("w_grouped", g))
+            cols = w_parts(g)[h]
+            interleave(engine, grouped[:, cols, :], w_raw[:, g, :, cols])
 
         def w_quant(engine, g, h):
-            grouped = live["w_grouped", g][:, halves(h), :].rearrange("p c t -> p (c t)")
-            quantize(w_codes[:, g, halves(h)], w_scales[:, g, halves(h)], grouped)
+            cols = w_parts(g)[h]
+            grouped = live["w_grouped", g][:, cols, :].rearrange("p c t -> p (c t)")
+            quantize(w_codes[:, g, cols], w_scales[:, g, cols], grouped)
 
         def wt_group(engine, i, h):
-            grouped = shared(("wt_grouped", i), [P, S, PACK], BF16, 1, "gpsimd_grouped" if i == 0 else "vector_grouped")
+            grouped = grouped_tile(("wt_grouped", i))
             interleave(engine, grouped[:, halves(h), :], wt_raw[:, i, :, halves(h)])
 
         def wt_quant(engine, i):
@@ -287,13 +344,12 @@ def tile_return_time_projection_h3_kernel(
                 words = pos_raw[:, g, c, :].bitcast(F32)
                 nc.tensor.transpose(bank[:, c, :], words[:, u : GROUP // 2 : 2], ident[:])
 
-        def pos_scale(engine, g, u):
-            pairs = live["pos_bank", g, u][:].rearrange("p c r -> p (c r)").bitcast(BF16)
-            for e in range(2):
-                t = 2 * u + e
-                nc.scalar.activation(
-                    out=pos_gain[:, g, t, :], in_=pairs[:, e : 2 * S : 2], func=ACT.Copy, scale=fgain[:, g, t : t + 1]
-                )
+        def pos_scale(engine, g, e):
+            pairs = live["pos_bank", g, e // 2][:].rearrange("p c r -> p (c r)").bitcast(BF16)[:, e % 2 : 2 * S : 2]
+            if engine == "scalar":
+                nc.scalar.activation(out=pos_gain[:, g, e, :], in_=pairs, func=ACT.Copy, scale=fgain[:, g, e : e + 1])
+            else:
+                nc.vector.tensor_scalar_mul(out=pos_gain[:, g, e, :], in0=pairs, scalar1=fgain[:, g, e : e + 1])
 
         def first(engine, n, s):
             b, g = UNITS[n]
@@ -378,6 +434,19 @@ def tile_return_time_projection_h3_kernel(
             for e in range(PACK):
                 nc.tensor.transpose(bank[:, e, :], live["y_turned", n][:, e, c * P : (c + 1) * P], ident[:])
 
+        def warm_up(engine, n, c):
+            bank = scalar_bank(("y_bank", n, c), [P, PACK, P])
+            for half in range(2):
+                nc.tensor.matmul_mx(
+                    out=bank[:].rearrange("p e m -> p (e m)")[:, halves(half)],
+                    lhsT=r_codes[:, 0, 0, 0:P].bitcast(FP8X4),
+                    lhsT_scale=r_scales[:, 0, 0, 0:P],
+                    rhs=w_codes[:, 0, halves(0)].bitcast(FP8X4),
+                    rhs_scale=w_scales[:, 0, halves(0)],
+                    start=True,
+                    stop=True,
+                )
+
         def y_copy(engine, n, c):
             rows = shared(("y_rows", n, c // 2), [P, 2, P, PACK], F32, 3)
             copy(engine, rows[:, c % 2, :, :], live["y_bank", n, c][:].rearrange("p e m -> p m e"))
@@ -391,9 +460,9 @@ def tile_return_time_projection_h3_kernel(
             )
 
         def y_group(engine, n, h):
-            tag = "gpsimd_grouped" if n < LAST else "vector_grouped"
-            grouped = shared(("y_grouped", n), [P, S, PACK], BF16, 1, tag)
-            interleave(engine, grouped[:, halves(h), :], live["y_turned", n][:, :, halves(h)])
+            grouped = grouped_tile(("y_grouped", n))
+            cols = y_parts(n)[h]
+            interleave(engine, grouped[:, cols, :], live["y_turned", n][:, :, cols])
 
         def y_quant(engine, n, k):
             b, g = UNITS[n]
@@ -417,21 +486,21 @@ def tile_return_time_projection_h3_kernel(
         lo, hi, whole = slice(0, 2), slice(2, 4), slice(0, 4)
         nc.vector.memset(gain_rows[:].bitcast(I32), 0)
         load_r(0, 0, lo)
-        load_w(0, halves(0))
         load_r(0, 0, hi)
-        load_w(0, halves(1))
+        load_w(0, halves(0))
         gain_hbm = time_gain.rearrange("(i c) -> i c", i=NI)
         nc.sync.dma_start(out=gain_rows[0 : 2 * NI : 2, :], in_=gain_hbm)
         nc.sync.dma_start(out=gain_rows[1 : 2 * NI : 2, 0 : GROUP - 2], in_=gain_hbm[:, 2:GROUP])
+        load_w(0, halves(1))
         load_r(0, 1, whole)
         load_wt(0)
         load_w(1, slice(0, GROUP))
-        load_r(1, 0, whole)
         nc.sync.dma_start(out=fgain_raw[:], in_=feat_gain.rearrange("(g p t) -> p g t", p=P, t=PACK))
+        load_r(1, 0, whole)
+        nc.sync.dma_start(out=gain[:], in_=time_gain.rearrange("(i p t) -> p i t", p=P, t=PACK))
         load_wt(1)
         load_r(1, 1, whole)
         load_pos(0)
-        nc.sync.dma_start(out=gain[:], in_=time_gain.rearrange("(i p t) -> p i t", p=P, t=PACK))
         load_w(2, slice(0, GROUP))
         load_pos(1)
         load_pos(2)
@@ -458,6 +527,7 @@ def tile_return_time_projection_h3_kernel(
             "h_quant": h_quant,
             "second": second,
             "finish": finish,
+            "warm": warm_up,
             "y_turn": y_turn,
             "y_copy": y_copy,
             "store_rows": store_rows,

from contextlib import ExitStack

import concourse.mybir as mybir
from concourse.masks import make_identity

B, T, D, F, S = 2, 1024, 512, 1536, 512
FLOPS = 2 * B * T * D * F + 2 * B * S * T * F

F32 = mybir.dt.float32
BF16 = mybir.dt.bfloat16
U32 = mybir.dt.uint32
I32 = mybir.dt.int32
U8 = mybir.dt.uint8
FP8X4 = mybir.dt.float8_e4m3fn_x4
ACT = mybir.ActivationFunctionType
ALU = mybir.AluOpType

P = 128
PACK = 4
GROUP = P * PACK
HALF = GROUP // 2
NG = F // GROUP
NI = T // GROUP
UNITS = [(b, g) for g in range(NG) for b in range(B)]
LAST = len(UNITS) - 1
SCALAR_BANKS = 5


def halves(h):
    return slice(h * HALF, (h + 1) * HALF)


def w_parts(g):
    return [halves(0), halves(1)] if g == 0 else [slice(0, GROUP)]


def y_parts(n):
    return [halves(0), halves(1)] if n >= LAST - 1 else [slice(0, S)]


def pieces(n):
    return [halves(0), halves(1)] if n == LAST else [slice(0, S)]


RELAY = [("wt_grouped", 0), ("w_grouped", 1), ("w_grouped", 2)] + [("y_grouped", n) for n in range(LAST - 1)]


def engine_orders():
    tensor, scalar, vector, gpsimd, sync = [], [], [], [], []

    def to_scalar(turn, read, *args):
        tensor.append((turn,) + args)
        scalar.append((read,) + args)

    def gelus(n, steps):
        for s in steps:
            if n <= LAST:
                to_scalar("first", "gelu", n, s)

    def r_pair(b, i):
        for tp in range(2):
            to_scalar("r_turn", "r_copy", b, i, tp)

    def pos_pair(g, u):
        tensor.append(("pos_turn", g, u))
        scalar.extend([("pos_scale", g, 2 * u), ("pos_scale", g, 2 * u + 1)])

    def y_pair(n, c):
        to_scalar("y_turn", "y_copy", n, c)
        to_scalar("y_turn", "y_copy", n, c + 1)
        sync.append(("store_rows", n, c, 2))

    def seconds(n, groups, k):
        tensor.extend([("second", n, e, k) for e in groups])

    def finishes(n, groups, k):
        vector.extend([("finish", n, e, k) for e in groups])

    tensor.append(("r_turn", 0, 0, 0))
    to_scalar("r_turn", "r_copy", 0, 0, 1)
    tensor.append(("gain_turn",))
    scalar.append(("w_group", 0, 1))
    gelus(0, [0, 1])
    r_pair(0, 1)
    gelus(0, [2, 3, 4, 5, 6, 7])
    r_pair(1, 0)
    to_scalar("r_turn", "r_copy", 1, 1, 0)
    scalar.append(("wt_group", 1, 1))
    to_scalar("r_turn", "r_copy", 1, 1, 1)
    gelus(1, [0, 1])
    tensor.append(("pos_turn", 0, 0))
    scalar.append(("pos_scale", 0, 0))
    gelus(1, [2, 3])
    pos_pair(0, 1)
    gelus(1, [4])
    vector.extend([("r_copy", 0, 0, 0), ("w_group", 0, 0), ("r_quant", 0, 0, 0), ("w_quant", 0, 0), ("r_quant", 0, 0, 1)])
    vector.extend([("w_quant", 0, 1), ("scale_time", 0, 0), ("wt_group", 0, 1), ("r_quant", 0, 1, 0), ("r_quant", 0, 1, 1)])
    vector.extend([("wt_quant", 0), ("fgain_cast",), ("scale_time", 0, 1), ("scale_time", 0, 2), ("scale_time", 0, 3)])
    vector.extend([("r_quant", 1, 0, 0), ("r_quant", 1, 0, 1), ("wt_group", 1, 0), ("h_quant", 0, 0), ("r_quant", 1, 1, 0)])
    vector.extend([("h_quant", 0, 1), ("wt_quant", 1), ("w_quant", 1, 0), ("r_quant", 1, 1, 1), ("pos_scale", 0, 1)])
    gpsimd.extend([("wt_group", 0, 0), ("w_group", 1, 0), ("w_group", 2, 0)])

    for n in range(1, LAST + 1):
        prev, late = n - 1, n - 2
        seconds(prev, [0, 1], 0)
        if n == 1:
            gelus(n, [5])
        elif n > 2:
            y_pair(late, 0)
        gelus(n, [6, 7])
        seconds(prev, [2, 3], 0)
        if n > 1:
            y_pair(late, 2)
        gelus(n + 1, [0, 1])
        if n < LAST:
            pos_pair((n + 1) // 2, (n + 1) % 2)
        gelus(n + 1, [2, 3])
        if n == 1:
            y_pair(prev, 0)
        gelus(n + 1, [4, 5])
        vector.append(("scale_time", n, 0))
        finishes(prev, [0, 1], 0)
        vector.append(("scale_time", n, 1))
        finishes(prev, [2, 3], 0)
        if n == LAST - 1:
            scalar.remove(("y_copy", late, 3))
            vector.append(("y_copy", late, 3))
        vector.extend([("scale_time", n, 3), ("h_quant", n, 0), ("h_quant", n, 1)])
        if n == 1:
            vector.append(("w_quant", 2, 0))
        else:
            gpsimd.append(("y_group", late, 0))
            vector.append(("y_quant", late, 0))
            sync.append(("store_words", late))
        gpsimd.append(("scale_time", n, 2))
        if n == 3:
            sync.append(("store_scales", 0))

    prev = LAST - 1
    sync.remove(("store_words", LAST - 2))
    y_pair(prev, 0)
    scalar.append(("y_group", prev, 1))
    sync.extend([("store_scales", 1), ("store_words", LAST - 2)])
    y_pair(prev, 2)
    tensor.remove(("y_turn", prev, 3))
    tensor.extend([("warm", prev, 3), ("warm", prev, 3), ("y_turn", prev, 3)])
    vector.append(("y_group", prev, 0))
    seconds(LAST, range(PACK), 0)
    finishes(LAST, range(PACK), 0)
    vector.append(("y_quant", prev, 0))
    gpsimd.append(("y_group", LAST, 0))
    seconds(LAST, range(PACK), 1)
    finishes(LAST, range(PACK), 1)
    tensor.extend([("y_turn", LAST, c) for c in range(PACK)])
    scalar.extend([("y_copy", LAST, c) for c in (0, 2, 3)])
    vector.extend([("y_copy", LAST, 1), ("y_group", LAST, 1), ("y_quant", LAST, 0), ("y_quant", LAST, 1)])
    sync.append(("store_words", prev))
    sync.extend([("store_rows", LAST, c, 1) for c in range(3)])
    sync.extend([("store_words", LAST), ("store_rows", LAST, 3, 1), ("store_scales", NG - 1)])
    return {"tensor": tensor, "scalar": scalar, "vector": vector, "gpsimd": gpsimd, "sync": sync}


def last_read(key):
    if key[0] == "w_grouped":
        return [("w_quant", key[1], h) for h in range(len(w_parts(key[1])))]
    if key[0] == "wt_grouped":
        return [("wt_quant", key[1])]
    return [("y_quant", key[1], k) for k in range(len(pieces(key[1])))]


def needs(step):
    name, args = step[0], step[1:]
    if name == "first":
        (b, g), s = UNITS[args[0]], args[1]
        return [("r_quant", b, s // 4, s % 2), ("w_quant", g, (s // 2) % len(w_parts(g)))]
    if name == "gelu":
        return [("first",) + args]
    if name == "scale_time":
        return [("gelu", args[0], 2 * args[1]), ("gelu", args[0], 2 * args[1] + 1), ("gain_turn",)]
    if name == "h_quant":
        return [("scale_time", args[0], 2 * args[1]), ("scale_time", args[0], 2 * args[1] + 1)]
    if name == "second":
        return [("h_quant", args[0], i) for i in range(NI)] + [("wt_quant", i) for i in range(NI)]
    if name == "finish":
        return [("second",) + args, ("pos_scale", UNITS[args[0]][1], args[1])]
    if name == "y_turn":
        return [("finish", args[0], e, args[1] * len(pieces(args[0])) // PACK) for e in range(PACK)]
    if name in ("w_group", "wt_group", "y_group"):
        key = (name + "ed", args[0])
        freed = last_read(RELAY[RELAY.index(key) - 1]) if key in RELAY[1:] else []
        if name != "y_group":
            return freed
        return freed + [("finish", args[0], e, args[1] * len(pieces(args[0])) // 2) for e in range(PACK)]
    if name == "warm":
        return [("r_quant", 0, 0, 0), ("w_quant", 0, 0)]
    if name == "y_quant":
        return [("y_group", args[0], args[1])] if args[0] == LAST else [("y_group", args[0], h) for h in range(len(y_parts(args[0])))]
    if name == "store_scales":
        return [("y_quant", n, len(pieces(n)) - 1) for n in range(LAST + 1) if UNITS[n][1] == args[0]]
    if name == "store_rows":
        return [("y_copy", args[0], args[1] + c) for c in range(args[2])]
    if name == "store_words":
        return [("y_quant", args[0], len(pieces(args[0])) - 1)]
    if name == "wt_quant":
        return [("wt_group", args[0], h) for h in range(2)]
    if name == "pos_scale":
        return [("pos_turn", args[0], args[1] // 2), ("fgain_cast",)]
    before = {
        "r_copy": "r_turn",
        "r_quant": "r_copy",
        "w_quant": "w_group",
        "y_copy": "y_turn",
    }
    return [(before[name],) + args] if name in before else []


def tile_return_time_projection_h3_kernel(
    tc, returns, w_in, time_gain, w_time, pos, feat_gain, out_0, out_1, out_2
):
    nc = tc.nc
    with ExitStack() as ctx:
        keep = ctx.enter_context(tc.tile_pool(name="keep", bufs=1))
        work = ctx.enter_context(tc.tile_pool(name="work", bufs=2))
        psum = ctx.enter_context(tc.psum_pool(name="psum", bufs=1))
        ctx.enter_context(tc.manual_schedule())

        ident = keep.tile([P, P], F32, name="ident")
        warm = keep.tile([P, 8], F32, name="warm")
        gain = keep.tile([P, NI, PACK], BF16, name="gain")
        fgain_raw = keep.tile([P, NG, PACK], BF16, name="fgain_raw")
        fgain = keep.tile([P, NG, PACK], F32, name="fgain")
        r_raw = keep.tile([P, B, NI, PACK, D], BF16, name="r_raw")
        w_raw = keep.tile([P, NG, PACK, GROUP], BF16, name="w_raw")
        wt_raw = keep.tile([P, NI, PACK, S], BF16, name="wt_raw")
        pos_raw = keep.tile([P, NG, PACK, GROUP], BF16, name="pos_raw")
        r_codes = keep.tile([P, B, NI, GROUP], U32, name="r_codes", align_bytes=64)
        r_scales = keep.tile([P, B, NI, GROUP], U8, name="r_scales", align_bytes=64)
        w_codes = keep.tile([P, NG, GROUP], U32, name="w_codes", align_bytes=64)
        w_scales = keep.tile([P, NG, GROUP], U8, name="w_scales", align_bytes=64)
        wt_codes = keep.tile([P, NI, S], U32, name="wt_codes", align_bytes=64)
        wt_scales = keep.tile([P, NI, S], U8, name="wt_scales", align_bytes=64)
        pos_gain = keep.tile([P, NG, PACK, S], F32, name="pos_gain")
        y_codes = keep.tile([P, NG, B, S], U32, name="y_codes", align_bytes=64)
        y_scales = keep.tile([P, NG, B, S], U8, name="y_scales", align_bytes=64)
        gain_rows = keep.tile([P, GROUP], BF16, name="gain_rows")
        gain_bank = psum.tile([P, P], F32, name="gain_bank")
        relay = keep.tile([P, GROUP, PACK], BF16, name="relay", align_bytes=64)
        live = {}

        def shared(key, shape, dtype, bufs, tag=None):
            if key not in live:
                live[key] = work.tile(shape, dtype, name=key[0], tag=tag or key[0], bufs=bufs, align_bytes=64)
            return live[key]

        def grouped_tile(key):
            if key in RELAY:
                live[key] = relay
            return shared(key, [P, GROUP, PACK], BF16, 2, "grouped")

        def scalar_bank(key, shape):
            if key not in live:
                live[key] = psum.tile(shape, F32, name="scalar_bank", bufs=SCALAR_BANKS)
            return live[key]

        def quantize(codes, scales, grouped):
            nc.vector.quantize_mx(out=codes.bitcast(FP8X4), scales=scales, in_=grouped)

        def interleave(engine, dst, src):
            dst_v = dst.rearrange("p (c i) t -> p c t i", i=PACK)
            src_v = src.rearrange("p t (c i) -> p c t i", i=PACK)
            if engine == "scalar":
                nc.scalar.copy(out=dst_v, in_=src_v)
            elif engine == "gpsimd":
                nc.gpsimd.tensor_scalar(out=dst_v, in0=src_v, scalar1=1.0, scalar2=1.0, op0=ALU.mult, op1=ALU.mult)
            else:
                nc.vector.tensor_copy(out=dst_v, in_=src_v)

        def copy(engine, dst, src):
            if engine == "scalar":
                nc.scalar.copy(out=dst, in_=src)
            else:
                nc.vector.tensor_copy(out=dst, in_=src)

        def load_r(b, i, tp):
            rows = returns[b, i * GROUP : (i + 1) * GROUP, :].rearrange("(p t) d -> p t d", t=PACK)
            nc.sync.dma_start(out=r_raw[:, b, i, tp, :], in_=rows[:, tp, :])

        def load_w(g, cols):
            rows = w_in[:, g * GROUP : (g + 1) * GROUP].rearrange("(p t) f -> p t f", t=PACK)
            nc.sync.dma_start(out=w_raw[:, g, :, cols], in_=rows[:, :, cols])

        def load_wt(i):
            rows = w_time[i * GROUP : (i + 1) * GROUP, :].rearrange("(p t) s -> p t s", t=PACK)
            nc.sync.dma_start(out=wt_raw[:, i, :, :], in_=rows)

        def load_pos(g):
            rows = pos[:, g * GROUP : (g + 1) * GROUP].rearrange("(c p) f -> p c f", p=P)
            nc.sync.dma_start(out=pos_raw[:, g, :, :], in_=rows)

        def fgain_cast(engine):
            copy(engine, fgain[:], fgain_raw[:])

        def gain_turn(engine):
            nc.tensor.transpose(gain_bank[:], gain_rows[:].bitcast(F32)[:, 0 : GROUP // 2 : 2], ident[:])

        def r_turn(engine, b, i, tp):
            bank = scalar_bank(("r_bank", b, i, tp), [P, 2, 2, P])
            for t in range(2):
                words = r_raw[:, b, i, 2 * tp + t, :].bitcast(F32)
                for u in range(2):
                    nc.tensor.transpose(bank[:, t, u, :], words[:, u : D // 2 : 2], ident[:])

        def r_copy(engine, b, i, tp):
            grouped = shared(("r_grouped", b, i, tp), [P, 2 * P * PACK], BF16, 3)
            copy(
                engine,
                grouped[:].bitcast(F32).rearrange("p (t r u) -> p t r u", t=2, u=2),
                live["r_bank", b, i, tp][:].rearrange("p t u r -> p t r u"),
            )

        def r_quant(engine, b, i, tp):
            quantize(r_codes[:, b, i, halves(tp)], r_scales[:, b, i, halves(tp)], live["r_grouped", b, i, tp][:])

        def w_group(engine, g, h):
            grouped = grouped_tile(("w_grouped", g))
            cols = w_parts(g)[h]
            interleave(engine, grouped[:, cols, :], w_raw[:, g, :, cols])

        def w_quant(engine, g, h):
            cols = w_parts(g)[h]
            grouped = live["w_grouped", g][:, cols, :].rearrange("p c t -> p (c t)")
            quantize(w_codes[:, g, cols], w_scales[:, g, cols], grouped)

        def wt_group(engine, i, h):
            grouped = grouped_tile(("wt_grouped", i))
            interleave(engine, grouped[:, halves(h), :], wt_raw[:, i, :, halves(h)])

        def wt_quant(engine, i):
            quantize(wt_codes[:, i, :], wt_scales[:, i, :], live["wt_grouped", i][:].rearrange("p c t -> p (c t)"))

        def pos_turn(engine, g, u):
            bank = scalar_bank(("pos_bank", g, u), [P, PACK, P])
            for c in range(PACK):
                words = pos_raw[:, g, c, :].bitcast(F32)
                nc.tensor.transpose(bank[:, c, :], words[:, u : GROUP // 2 : 2], ident[:])

        def pos_scale(engine, g, e):
            pairs = live["pos_bank", g, e // 2][:].rearrange("p c r -> p (c r)").bitcast(BF16)[:, e % 2 : 2 * S : 2]
            if engine == "scalar":
                nc.scalar.activation(out=pos_gain[:, g, e, :], in_=pairs, func=ACT.Copy, scale=fgain[:, g, e : e + 1])
            else:
                nc.vector.tensor_scalar_mul(out=pos_gain[:, g, e, :], in0=pairs, scalar1=fgain[:, g, e : e + 1])

        def first(engine, n, s):
            b, g = UNITS[n]
            i, h, tp = s // 4, (s // 2) % 2, s % 2
            bank = scalar_bank(("first_bank", n, s), [P, 2, HALF])
            for t in range(2):
                rows = slice((2 * tp + t) * P, (2 * tp + t + 1) * P)
                nc.tensor.matmul_mx(
                    out=bank[:, t, :],
                    lhsT=r_codes[:, b, i, rows].bitcast(FP8X4),
                    lhsT_scale=r_scales[:, b, i, rows],
                    rhs=w_codes[:, g, halves(h)].bitcast(FP8X4),
                    rhs_scale=w_scales[:, g, halves(h)],
                    start=True,
                    stop=True,
                )

        def gelu(engine, n, s):
            act = shared(("act", n, s // 2), [P, 2, HALF, 2], F32, 6)
            nc.scalar.activation(
                out=act[:, s % 2, :, :].rearrange("p (e m) t -> p e m t", e=PACK),
                in_=live["first_bank", n, s][:].rearrange("p t (m e) -> p e m t", e=PACK),
                func=ACT.Gelu_apprx_tanh,
            )

        def scale_time(engine, n, q):
            i, h = q // 2, q % 2
            grouped = shared(("h_grouped", n, i), [P, PACK, P, PACK], BF16, 3)
            m = P // 2
            if engine == "gpsimd":
                gain_v = gain[:, i, :].rearrange("p (a t) -> p a t", a=2)
                multiply = nc.gpsimd.tensor_tensor
            else:
                gain_v = gain_bank[:].bitcast(BF16)[:, PACK * i : PACK * (i + 1)].rearrange("p (a t) -> p a t", a=2)
                multiply = nc.vector.tensor_tensor
            multiply(
                out=grouped[:, :, h * m : (h + 1) * m, :].rearrange("p e m (a t) -> p e m a t", a=2),
                in0=live["act", n, q][:].rearrange("p a (e m) t -> p e m a t", e=PACK),
                in1=gain_v.unsqueeze(1).unsqueeze(1).to_broadcast([P, PACK, m, 2, 2]),
                op=ALU.mult,
            )

        def h_quant(engine, n, i):
            codes = shared(("h_codes", n, i), [P, GROUP], U32, 4)
            scales = shared(("h_scales", n, i), [P, GROUP], U8, 4)
            quantize(codes[:], scales[:], live["h_grouped", n, i][:].rearrange("p e m t -> p (e m t)"))

        def second(engine, n, e, k):
            cols = pieces(n)[k]
            if n == LAST and e >= 2:
                bank = scalar_bank(("second_bank", n, e, k), [P, HALF])
            else:
                bank = psum.tile([P, cols.stop - cols.start], F32, name="second_bank", bufs=2)
            rows = slice(e * P, (e + 1) * P)
            for i in range(NI):
                nc.tensor.matmul_mx(
                    out=bank[:],
                    lhsT=live["h_codes", n, i][:, rows].bitcast(FP8X4),
                    lhsT_scale=live["h_scales", n, i][:, rows],
                    rhs=wt_codes[:, i, cols].bitcast(FP8X4),
                    rhs_scale=wt_scales[:, i, cols],
                    start=(i == 0),
                    stop=(i == NI - 1),
                )
            live["second_bank", n, e, k] = bank

        def finish(engine, n, e, k):
            g = UNITS[n][1]
            cols = pieces(n)[k]
            turned = shared(("y_turned", n), [P, PACK, S], F32, 3)
            nc.vector.scalar_tensor_tensor(
                out=turned[:, e, cols],
                in0=live["second_bank", n, e, k][:],
                scalar=fgain[:, g, e : e + 1],
                in1=pos_gain[:, g, e, cols],
                op0=ALU.mult,
                op1=ALU.add,
            )

        def y_turn(engine, n, c):
            bank = scalar_bank(("y_bank", n, c), [P, PACK, P])
            for e in range(PACK):
                nc.tensor.transpose(bank[:, e, :], live["y_turned", n][:, e, c * P : (c + 1) * P], ident[:])

        def warm_up(engine, n, c):
            bank = scalar_bank(("y_bank", n, c), [P, PACK, P])
            for half in range(2):
                nc.tensor.matmul_mx(
                    out=bank[:].rearrange("p e m -> p (e m)")[:, halves(half)],
                    lhsT=r_codes[:, 0, 0, 0:P].bitcast(FP8X4),
                    lhsT_scale=r_scales[:, 0, 0, 0:P],
                    rhs=w_codes[:, 0, halves(0)].bitcast(FP8X4),
                    rhs_scale=w_scales[:, 0, halves(0)],
                    start=True,
                    stop=True,
                )

        def y_copy(engine, n, c):
            rows = shared(("y_rows", n, c // 2), [P, 2, P, PACK], F32, 3)
            copy(engine, rows[:, c % 2, :, :], live["y_bank", n, c][:].rearrange("p e m -> p m e"))

        def store_rows(engine, n, c, count):
            b, g = UNITS[n]
            rows = out_0[b, c * P : (c + count) * P, g * GROUP : (g + 1) * GROUP]
            nc.sync.dma_start(
                out=rows.rearrange("(c p) f -> p c f", p=P),
                in_=live["y_rows", n, c // 2][:, c % 2 : c % 2 + count, :, :].rearrange("p c m e -> p c (m e)"),
            )

        def y_group(engine, n, h):
            grouped = grouped_tile(("y_grouped", n))
            cols = y_parts(n)[h]
            interleave(engine, grouped[:, cols, :], live["y_turned", n][:, :, cols])

        def y_quant(engine, n, k):
            b, g = UNITS[n]
            cols = pieces(n)[k]
            grouped = live["y_grouped", n][:, cols, :].rearrange("p c t -> p (c t)")
            quantize(y_codes[:, g, b, cols], y_scales[:, g, b, cols], grouped)

        def store_words(engine, n):
            b, g = UNITS[n]
            words = out_1[g].rearrange("p m t -> p (m t)").bitcast(I32)
            nc.sync.dma_start(out=words[:, b * S : (b + 1) * S], in_=y_codes[:, g, b, :].bitcast(I32))

        def store_scales(engine, g):
            rows = out_2[g].bitcast(I32)
            for q in range(4):
                nc.sync.dma_start(
                    out=rows[4 * q : 4 * q + 4, :],
                    in_=y_scales[32 * q : 32 * q + 4, g, :, :].rearrange("p b s -> p (b s)").bitcast(I32),
                )

        lo, hi, whole = slice(0, 2), slice(2, 4), slice(0, 4)
        nc.vector.memset(gain_rows[:].bitcast(I32), 0)
        load_r(0, 0, lo)
        load_r(0, 0, hi)
        load_w(0, halves(0))
        gain_hbm = time_gain.rearrange("(i c) -> i c", i=NI)
        nc.sync.dma_start(out=gain_rows[0 : 2 * NI : 2, :], in_=gain_hbm)
        nc.sync.dma_start(out=gain_rows[1 : 2 * NI : 2, 0 : GROUP - 2], in_=gain_hbm[:, 2:GROUP])
        load_w(0, halves(1))
        load_r(0, 1, whole)
        load_wt(0)
        load_w(1, slice(0, GROUP))
        nc.sync.dma_start(out=fgain_raw[:], in_=feat_gain.rearrange("(g p t) -> p g t", p=P, t=PACK))
        load_r(1, 0, whole)
        nc.sync.dma_start(out=gain[:], in_=time_gain.rearrange("(i p t) -> p i t", p=P, t=PACK))
        load_wt(1)
        load_r(1, 1, whole)
        load_pos(0)
        load_w(2, slice(0, GROUP))
        load_pos(1)
        load_pos(2)

        make_identity(nc, ident[:])
        nc.vector.memset(warm[:], 0.0)
        nc.scalar.activation(out=warm[:, 0:1], in_=warm[:, 1:2], func=ACT.Gelu_apprx_tanh)

        emit = {
            "fgain_cast": fgain_cast,
            "gain_turn": gain_turn,
            "r_turn": r_turn,
            "r_copy": r_copy,
            "r_quant": r_quant,
            "w_group": w_group,
            "w_quant": w_quant,
            "wt_group": wt_group,
            "wt_quant": wt_quant,
            "pos_turn": pos_turn,
            "pos_scale": pos_scale,
            "first": first,
            "gelu": gelu,
            "scale_time": scale_time,
            "h_quant": h_quant,
            "second": second,
            "finish": finish,
            "warm": warm_up,
            "y_turn": y_turn,
            "y_copy": y_copy,
            "store_rows": store_rows,
            "y_group": y_group,
            "y_quant": y_quant,
            "store_words": store_words,
            "store_scales": store_scales,
        }
        queues = engine_orders()
        written = set()
        while any(queues.values()):
            moved = False
            for engine, queue in queues.items():
                while queue and all(need in written for need in needs(queue[0])):
                    step = queue[0]
                    queue.remove(step)
                    emit[step[0]](engine, *step[1:])
                    written.add(step)
                    moved = True
            assert moved
